import numpy as np
import ml_dtypes

BF16 = ml_dtypes.bfloat16


def bf(x):
    return np.asarray(x, np.float32).astype(BF16)


def f32(x):
    return np.asarray(x, np.float32)


def f64(x):
    return np.asarray(x).astype(np.float64)


def striped(idx):
    return np.concatenate([l.reshape(-1, 16).T for l in idx])


def rows(idx, k):
    return np.tile(np.repeat(idx, 16, axis=0), (k // (16 * 8), 1))


def look(tab, idx):
    return np.take_along_axis(f64(tab), rows(idx, len(tab)), axis=1)


K, S, V, N, M = 256, 2048, 1024, 1024, 256


def setup_inputs():
    return {"tab": f32(np.random.standard_normal((2, K, S))), "y": f32(np.random.standard_normal((K, V))), "w": bf(np.random.standard_normal((K, M)) / np.sqrt(K)), "b": f32(0.5 * np.random.standard_normal((M, 1))), "offs": striped(np.stack([np.random.permutation(S)[:N] for _ in range(8)]))}


def reference(tab, y, w, b, offs):
    idx = np.stack([g.T.reshape(-1) for g in np.split(offs, 8)])
    x = (look(tab[0], idx) + f64(y)) * (np.maximum(look(tab[1], idx), 0.0))
    return np.maximum(f64(w).T @ x + f64(b), 0.0)

@@ -1,0 +1,66 @@
+import concourse.mybir as mybir
+
+FLOPS = 2 * 256 * 256 * 1024
+
+BF16, F32, U16 = mybir.dt.bfloat16, mybir.dt.float32, mybir.dt.uint16
+ADD, MULT = mybir.AluOpType.add, mybir.AluOpType.mult
+RELU = mybir.ActivationFunctionType.Relu
+
+P = 128
+PIECE = 512
+
+
+def tile_lookup_vg_addrelu_relu_kernel(tc, tab, y, w, b, offs, out):
+    nc = tc.nc
+    rows, places = tab.shape[1], tab.shape[2]
+    n, m = y.shape[1], w.shape[1]
+    row_blocks, out_blocks, pieces = rows // P, m // P, n // PIECE
+    list_columns = PIECE // 16
+
+    with (
+        tc.tile_pool(name="held", bufs=1) as held,
+        tc.tile_pool(name="work", bufs=3) as work,
+        tc.psum_pool(name="psum", bufs=1) as psum,
+    ):
+        offsets = held.tile([P, n // 16], U16, name="offsets")
+        values = [held.tile([P, places], F32, name=f"values{k}") for k in range(row_blocks)]
+        gates = [held.tile([P, places], F32, name=f"gates{k}") for k in range(row_blocks)]
+        stream = [held.tile([P, n], F32, name=f"stream{k}") for k in range(row_blocks)]
+        weights = held.tile([P, row_blocks, m], BF16, name="weights")
+        bias = held.tile([P, out_blocks], F32, name="bias")
+
+        nc.sync.dma_start(offsets[:], offs)
+        for k in range(row_blocks):
+            block = slice(k * P, (k + 1) * P)
+            nc.sync.dma_start(values[k][:], tab[0, block, :])
+            nc.sync.dma_start(stream[k][:], y[block, :])
+            nc.sync.dma_start(gates[k][:], tab[1, block, :])
+        nc.gpsimd.dma_start(weights[:], w.rearrange("(k p) m -> p k m", p=P))
+        with nc.allow_non_contiguous_dma(reason="the bias has one value for each partition"):
+            nc.gpsimd.dma_start(bias[:], b.rearrange("(o p) one -> p (o one)", p=P))
+
+        banks = [[psum.tile([P, PIECE], F32, name=f"bank{o}_{c}") for c in range(pieces)] for o in range(out_blocks)]
+        for k in range(row_blocks):
+            for c in range(pieces):
+                piece = slice(c * PIECE, (c + 1) * PIECE)
+                entries = offsets[:, c * list_columns : (c + 1) * list_columns]
+                total = work.tile([P, PIECE], F32, name="total")
+                nc.vector.tensor_tensor(total[:], values[k][:].indirect(entries), stream[k][:, piece], ADD)
+                gate = work.tile([P, PIECE], F32, name="gate")
+                nc.scalar.activation(gate[:], gates[k][:].indirect(entries), RELU)
+                x = work.tile([P, PIECE], BF16, name="x")
+                nc.vector.tensor_tensor(x[:], total[:], gate[:], MULT)
+                for o in range(out_blocks):
+                    nc.tensor.matmul(
+                        banks[o][c][:],
+                        weights[:, k, o * P : (o + 1) * P],
+                        x[:],
+                        start=k == 0,
+                        stop=k == row_blocks - 1,
+                    )
+
+        for c in range(pieces):
+            for o in range(out_blocks):
+                result = work.tile([P, PIECE], F32, name="result")
+                nc.scalar.activation(result[:], banks[o][c][:], RELU, bias=bias[:, o : o + 1])
+                nc.sync.dma_start(out[o * P : (o + 1) * P, c * PIECE : (c + 1) * PIECE], result[:])

@@ -3,7 +3,7 @@ import concourse.mybir as mybir
 FLOPS = 2 * 256 * 256 * 1024
 
 BF16, F32, U16 = mybir.dt.bfloat16, mybir.dt.float32, mybir.dt.uint16
-ADD, MULT = mybir.AluOpType.add, mybir.AluOpType.mult
+ADD, MULT, MAX = mybir.AluOpType.add, mybir.AluOpType.mult, mybir.AluOpType.max
 RELU = mybir.ActivationFunctionType.Relu
 
 P = 128
@@ -19,7 +19,7 @@ def tile_lookup_vg_addrelu_relu_kernel(tc, tab, y, w, b, offs, out):
 
     with (
         tc.tile_pool(name="held", bufs=1) as held,
-        tc.tile_pool(name="work", bufs=3) as work,
+        tc.tile_pool(name="work", bufs=4) as work,
         tc.psum_pool(name="psum", bufs=1) as psum,
     ):
         offsets = held.tile([P, n // 16], U16, name="offsets")
@@ -35,9 +35,9 @@ def tile_lookup_vg_addrelu_relu_kernel(tc, tab, y, w, b, offs, out):
             nc.sync.dma_start(values[k][:], tab[0, block, :])
             nc.sync.dma_start(stream[k][:], y[block, :])
             nc.sync.dma_start(gates[k][:], tab[1, block, :])
-        nc.gpsimd.dma_start(weights[:], w.rearrange("(k p) m -> p k m", p=P))
+        nc.scalar.dma_start(weights[:], w.rearrange("(k p) m -> p k m", p=P))
         with nc.allow_non_contiguous_dma(reason="the bias has one value for each partition"):
-            nc.gpsimd.dma_start(bias[:], b.rearrange("(o p) one -> p (o one)", p=P))
+            nc.scalar.dma_start(bias[:], b.rearrange("(o p) one -> p (o one)", p=P))
 
         banks = [[psum.tile([P, PIECE], F32, name=f"bank{o}_{c}") for c in range(pieces)] for o in range(out_blocks)]
         for k in range(row_blocks):
@@ -62,5 +62,8 @@ def tile_lookup_vg_addrelu_relu_kernel(tc, tab, y, w, b, offs, out):
         for c in range(pieces):
             for o in range(out_blocks):
                 result = work.tile([P, PIECE], F32, name="result")
-                nc.scalar.activation(result[:], banks[o][c][:], RELU, bias=bias[:, o : o + 1])
+                if o % 2 == 0:
+                    nc.scalar.activation(result[:], banks[o][c][:], RELU, bias=bias[:, o : o + 1])
+                else:
+                    nc.vector.tensor_scalar(result[:], banks[o][c][:], bias[:, o : o + 1], 0.0, ADD, MAX)
                 nc.sync.dma_start(out[o * P : (o + 1) * P, c * PIECE : (c + 1) * PIECE], result[:])

@@ -25,7 +25,7 @@ def tile_lookup_vg_addrelu_relu_kernel(tc, tab, y, w, b, offs, out):
         offsets = held.tile([P, n // 16], U16, name="offsets")
         values = [held.tile([P, places], F32, name=f"values{k}") for k in range(row_blocks)]
         gates = [held.tile([P, places], F32, name=f"gates{k}") for k in range(row_blocks)]
-        stream = [held.tile([P, n], F32, name=f"stream{k}") for k in range(row_blocks)]
+        stream = [[held.tile([P, PIECE], F32, name=f"stream{k}_{c}") for c in range(pieces)] for k in range(row_blocks)]
         weights = held.tile([P, row_blocks, m], BF16, name="weights")
         bias = held.tile([P, out_blocks], F32, name="bias")
 
@@ -33,19 +33,20 @@ def tile_lookup_vg_addrelu_relu_kernel(tc, tab, y, w, b, offs, out):
         for k in range(row_blocks):
             block = slice(k * P, (k + 1) * P)
             nc.sync.dma_start(values[k][:], tab[0, block, :])
-            nc.sync.dma_start(stream[k][:], y[block, :])
+            nc.sync.dma_start(stream[k][0][:], y[block, 0:PIECE])
             nc.sync.dma_start(gates[k][:], tab[1, block, :])
+            for c in range(1, pieces):
+                nc.sync.dma_start(stream[k][c][:], y[block, c * PIECE : (c + 1) * PIECE])
         nc.scalar.dma_start(weights[:], w.rearrange("(k p) m -> p k m", p=P))
         with nc.allow_non_contiguous_dma(reason="the bias has one value for each partition"):
-            nc.scalar.dma_start(bias[:], b.rearrange("(o p) one -> p (o one)", p=P))
+            nc.sync.dma_start(bias[:], b.rearrange("(o p) one -> p (o one)", p=P))
 
         banks = [[psum.tile([P, PIECE], F32, name=f"bank{o}_{c}") for c in range(pieces)] for o in range(out_blocks)]
         for k in range(row_blocks):
             for c in range(pieces):
-                piece = slice(c * PIECE, (c + 1) * PIECE)
                 entries = offsets[:, c * list_columns : (c + 1) * list_columns]
                 total = work.tile([P, PIECE], F32, name="total")
-                nc.vector.tensor_tensor(total[:], values[k][:].indirect(entries), stream[k][:, piece], ADD)
+                nc.vector.tensor_tensor(total[:], values[k][:].indirect(entries), stream[k][c][:], ADD)
                 gate = work.tile([P, PIECE], F32, name="gate")
                 nc.scalar.activation(gate[:], gates[k][:].indirect(entries), RELU)
                 x = work.tile([P, PIECE], BF16, name="x")

@@ -8,6 +8,8 @@ RELU = mybir.ActivationFunctionType.Relu
 
 P = 128
 PIECE = 512
+HALVES = 2
+HALF = PIECE // HALVES
 
 
 def tile_lookup_vg_addrelu_relu_kernel(tc, tab, y, w, b, offs, out):
@@ -19,7 +21,7 @@ def tile_lookup_vg_addrelu_relu_kernel(tc, tab, y, w, b, offs, out):
 
     with (
         tc.tile_pool(name="held", bufs=1) as held,
-        tc.tile_pool(name="work", bufs=4) as work,
+        tc.tile_pool(name="work", bufs=8) as work,
         tc.psum_pool(name="psum", bufs=1) as psum,
     ):
         offsets = held.tile([P, n // 16], U16, name="offsets")
@@ -41,7 +43,9 @@ def tile_lookup_vg_addrelu_relu_kernel(tc, tab, y, w, b, offs, out):
         with nc.allow_non_contiguous_dma(reason="the bias has one value for each partition"):
             nc.sync.dma_start(bias[:], b.rearrange("(o p) one -> p (o one)", p=P))
 
-        banks = [[psum.tile([P, PIECE], F32, name=f"bank{o}_{c}") for c in range(pieces)] for o in range(out_blocks)]
+        banks = [
+            [psum.tile([P, HALF], F32, name=f"bank{o}_{i}") for i in range(pieces * HALVES)] for o in range(out_blocks)
+        ]
         for k in range(row_blocks):
             for c in range(pieces):
                 entries = offsets[:, c * list_columns : (c + 1) * list_columns]
@@ -49,22 +53,24 @@ def tile_lookup_vg_addrelu_relu_kernel(tc, tab, y, w, b, offs, out):
                 nc.vector.tensor_tensor(total[:], values[k][:].indirect(entries), stream[k][c][:], ADD)
                 gate = work.tile([P, PIECE], F32, name="gate")
                 nc.scalar.activation(gate[:], gates[k][:].indirect(entries), RELU)
-                x = work.tile([P, PIECE], BF16, name="x")
-                nc.vector.tensor_tensor(x[:], total[:], gate[:], MULT)
-                for o in range(out_blocks):
-                    nc.tensor.matmul(
-                        banks[o][c][:],
-                        weights[:, k, o * P : (o + 1) * P],
-                        x[:],
-                        start=k == 0,
-                        stop=k == row_blocks - 1,
-                    )
+                for h in range(HALVES):
+                    half = slice(h * HALF, (h + 1) * HALF)
+                    x = work.tile([P, HALF], BF16, name="x")
+                    nc.vector.tensor_tensor(x[:], total[:, half], gate[:, half], MULT)
+                    for o in range(out_blocks):
+                        nc.tensor.matmul(
+                            banks[o][c * HALVES + h][:],
+                            weights[:, k, o * P : (o + 1) * P],
+                            x[:],
+                            start=k == 0,
+                            stop=k == row_blocks - 1,
+                        )
 
-        for c in range(pieces):
+        for i in range(pieces * HALVES):
             for o in range(out_blocks):
-                result = work.tile([P, PIECE], F32, name="result")
+                result = work.tile([P, HALF], F32, name="result")
                 if o % 2 == 0:
-                    nc.scalar.activation(result[:], banks[o][c][:], RELU, bias=bias[:, o : o + 1])
+                    nc.scalar.activation(result[:], banks[o][i][:], RELU, bias=bias[:, o : o + 1])
                 else:
-                    nc.vector.tensor_scalar(result[:], banks[o][c][:], bias[:, o : o + 1], 0.0, ADD, MAX)
-                nc.sync.dma_start(out[o * P : (o + 1) * P, c * PIECE : (c + 1) * PIECE], result[:])
+                    nc.vector.tensor_scalar(result[:], banks[o][i][:], bias[:, o : o + 1], 0.0, ADD, MAX)
+                nc.sync.dma_start(out[o * P : (o + 1) * P, i * HALF : (i + 1) * HALF], result[:])

@@ -41,7 +41,7 @@ def tile_lookup_vg_addrelu_relu_kernel(tc, tab, y, w, b, offs, out):
                 nc.sync.dma_start(stream[k][c][:], y[block, c * PIECE : (c + 1) * PIECE])
         nc.scalar.dma_start(weights[:], w.rearrange("(k p) m -> p k m", p=P))
         with nc.allow_non_contiguous_dma(reason="the bias has one value for each partition"):
-            nc.sync.dma_start(bias[:], b.rearrange("(o p) one -> p (o one)", p=P))
+            nc.scalar.dma_start(bias[:], b.rearrange("(o p) one -> p (o one)", p=P))
 
         banks = [
             [psum.tile([P, HALF], F32, name=f"bank{o}_{i}") for i in range(pieces * HALVES)] for o in range(out_blocks)

import concourse.mybir as mybir

FLOPS = 2 * 256 * 256 * 1024

BF16, F32, U16 = mybir.dt.bfloat16, mybir.dt.float32, mybir.dt.uint16
ADD, MULT, MAX = mybir.AluOpType.add, mybir.AluOpType.mult, mybir.AluOpType.max
RELU = mybir.ActivationFunctionType.Relu

P = 128
PIECE = 512
HALVES = 2
HALF = PIECE // HALVES


def tile_lookup_vg_addrelu_relu_kernel(tc, tab, y, w, b, offs, out):
    nc = tc.nc
    rows, places = tab.shape[1], tab.shape[2]
    n, m = y.shape[1], w.shape[1]
    row_blocks, out_blocks, pieces = rows // P, m // P, n // PIECE
    list_columns = PIECE // 16

    with (
        tc.tile_pool(name="held", bufs=1) as held,
        tc.tile_pool(name="work", bufs=8) as work,
        tc.psum_pool(name="psum", bufs=1) as psum,
    ):
        offsets = held.tile([P, n // 16], U16, name="offsets")
        values = [held.tile([P, places], F32, name=f"values{k}") for k in range(row_blocks)]
        gates = [held.tile([P, places], F32, name=f"gates{k}") for k in range(row_blocks)]
        stream = [[held.tile([P, PIECE], F32, name=f"stream{k}_{c}") for c in range(pieces)] for k in range(row_blocks)]
        weights = held.tile([P, row_blocks, m], BF16, name="weights")
        bias = held.tile([P, out_blocks], F32, name="bias")

        nc.sync.dma_start(offsets[:], offs)
        for k in range(row_blocks):
            block = slice(k * P, (k + 1) * P)
            nc.sync.dma_start(values[k][:], tab[0, block, :])
            nc.sync.dma_start(stream[k][0][:], y[block, 0:PIECE])
            nc.sync.dma_start(gates[k][:], tab[1, block, :])
            for c in range(1, pieces):
                nc.sync.dma_start(stream[k][c][:], y[block, c * PIECE : (c + 1) * PIECE])
        nc.scalar.dma_start(weights[:], w.rearrange("(k p) m -> p k m", p=P))
        with nc.allow_non_contiguous_dma(reason="the bias has one value for each partition"):
            nc.scalar.dma_start(bias[:], b.rearrange("(o p) one -> p (o one)", p=P))

        banks = [
            [psum.tile([P, HALF], F32, name=f"bank{o}_{i}") for i in range(pieces * HALVES)] for o in range(out_blocks)
        ]
        for k in range(row_blocks):
            for c in range(pieces):
                entries = offsets[:, c * list_columns : (c + 1) * list_columns]
                total = work.tile([P, PIECE], F32, name="total")
                nc.vector.tensor_tensor(total[:], values[k][:].indirect(entries), stream[k][c][:], ADD)
                gate = work.tile([P, PIECE], F32, name="gate")
                nc.scalar.activation(gate[:], gates[k][:].indirect(entries), RELU)
                for h in range(HALVES):
                    half = slice(h * HALF, (h + 1) * HALF)
                    x = work.tile([P, HALF], BF16, name="x")
                    nc.vector.tensor_tensor(x[:], total[:, half], gate[:, half], MULT)
                    for o in range(out_blocks):
                        nc.tensor.matmul(
                            banks[o][c * HALVES + h][:],
                            weights[:, k, o * P : (o + 1) * P],
                            x[:],
                            start=k == 0,
                            stop=k == row_blocks - 1,
                        )

        for i in range(pieces * HALVES):
            for o in range(out_blocks):
                result = work.tile([P, HALF], F32, name="result")
                if o % 2 == 0:
                    nc.scalar.activation(result[:], banks[o][i][:], RELU, bias=bias[:, o : o + 1])
                else:
                    nc.vector.tensor_scalar(result[:], banks[o][i][:], bias[:, o : o + 1], 0.0, ADD, MAX)
                nc.sync.dma_start(out[o * P : (o + 1) * P, i * HALF : (i + 1) * HALF], result[:])
